import numpy as np
import ml_dtypes


def mxq(x, axis, fmt="e4m3"):
    dtype, down = {"e4m3": (ml_dtypes.float8_e4m3fn, 7), "e5m2": (ml_dtypes.float8_e5m2, 14)}[fmt]
    v = np.moveaxis(np.asarray(x, np.float32).astype(ml_dtypes.bfloat16).astype(np.float64), axis, -1)
    blocks = v.reshape(v.shape[:-1] + (-1, 32))
    amax = np.abs(blocks).max(-1, keepdims=True)
    byte = np.maximum(np.where(amax > 0, np.frexp(amax)[1] - 1 + 127, 0) - down, 1)
    scale = np.exp2(byte - 127.0)
    codes = (blocks / scale).astype(np.float32).astype(dtype).astype(np.float64)
    return np.moveaxis((codes * scale).reshape(v.shape), -1, axis)


WIDE = False


def mx_kscale(k):
    if not WIDE:
        return np.ones(k)
    levels = np.array([10, -10, 5, -5, 0])
    if k % 512:
        return np.exp2(np.random.permutation(np.resize(levels, k // 32))).repeat(32)
    a = np.empty((k // 512, 16))
    for p in range(k // 512):
        a[p, :8] = np.random.permutation(np.resize(levels, 8))
        for g in range(8):
            far = levels[np.abs(levels - a[p, g]) >= 10]
            a[p, g + 8] = far[np.random.randint(len(far))]
    return np.exp2(a.ravel()).repeat(32)


def f64(x):
    return np.asarray(x).astype(np.float64)


def striped(idx):
    return np.tile(np.asarray(idx).reshape(-1, 16).T, (8, 1)).astype(np.uint16)


def unstriped(offs):
    return offs[:16].T.reshape(-1).astype(np.int64)


E2M1 = np.array([0.0, 0.5, 1.0, 1.5, 2.0, 3.0, 4.0, 6.0, -0.0, -0.5, -1.0, -1.5, -2.0, -3.0, -4.0, -6.0])


def pack_weight(w, fmt):
    k, n = w.shape
    w = f64(np.asarray(w, np.float32).astype(ml_dtypes.bfloat16)).reshape(k // 32, 32, n)
    amax = np.abs(w).max(1)
    if fmt == "e4m3":
        byte = np.frexp(amax)[1] - 1 + 127 - 7
    else:
        mant, ex = np.frexp(amax / 6.0)
        byte = np.where(mant > 0.5, ex, ex - 1) + 127
    byte = np.clip(np.where(amax > 0, byte, 1), 1, 254)
    scaled = (w * np.exp2(127.0 - byte)[:, None, :]).reshape(k, n).astype(np.float32)
    by_word = np.ascontiguousarray(scaled.reshape(k // 512, 128, 4, n).transpose(0, 1, 3, 2))
    if fmt == "e4m3":
        words = by_word.astype(ml_dtypes.float8_e4m3fn).view(np.uint8)
    else:
        c = by_word.astype(ml_dtypes.float4_e2m1fn).view(np.uint8) & 0xF
        words = (c[..., 0::2] | (c[..., 1::2] << 4)).reshape(k // 512, 128, 2 * n)
    return np.ascontiguousarray(words), np.ascontiguousarray(byte.astype(np.uint8).reshape(k // 512, 16, n))


def unpack_weight(words, scales, fmt):
    g, _, n = scales.shape
    words = np.ascontiguousarray(words).reshape(g, 128, n, -1)
    if fmt == "e4m3":
        vals = words.view(ml_dtypes.float8_e4m3fn).astype(np.float64)
    else:
        nib = np.empty((g, 128, n, 4), np.uint8)
        nib[..., 0::2] = words & 0xF
        nib[..., 1::2] = words >> 4
        vals = E2M1[nib]
    vals = vals * np.repeat(np.exp2(scales.astype(np.float64) - 127.0), 8, axis=1)[..., None]
    return vals.transpose(0, 1, 3, 2).reshape(g * 512, n)


def bf(x):
    return np.asarray(x, np.float32).astype(ml_dtypes.bfloat16)


def planes(Y):
    r, m = Y.shape
    b = f64(bf(Y)).reshape(r // 32, 32, m)
    amax = np.abs(b).max(1)
    byte = np.clip(np.where(amax > 0, np.frexp(amax)[1] - 1 + 127 - 7, 1), 1, 254)
    codes = (b * np.exp2(127.0 - byte)[:, None, :]).reshape(r, m).astype(np.float32).astype(ml_dtypes.float8_e4m3fn).view(np.uint8)
    words = codes.reshape(r // 512, 128, 4, m).transpose(0, 1, 3, 2)
    return np.ascontiguousarray(words), np.ascontiguousarray(byte.astype(np.uint8).reshape(r // 512, 16, m))


D, E, T, I, K, Q = 512, 512, 1024, 512, 512, 256


def setup_inputs():
    n = np.random.standard_normal
    idx = np.random.permutation(T)[:I]
    fd = mx_kscale(D)
    fe = mx_kscale(E)
    fi = mx_kscale(I)
    ti = np.ones(T)
    ti[idx] = fi
    fkeysp = pack_weight(n((D, T)) / fd[:, None], "e4m3")
    return {
        "fquery": (n((D, Q)) * 0.5 / np.sqrt(D) * fd[:, None]).astype(np.float32),
        "fkeys_words": fkeysp[0],
        "fkeys_scales": fkeysp[1],
        "gout": (n((E, Q)) * 1 / np.sqrt(E) * fe[:, None]).astype(np.float32),
        "vals": (n((E, T)) / fe[:, None]).astype(np.float32),
        "lse": (np.random.uniform(6.8, 7.2, (Q, 1))).astype(np.float32),
        "delta": (np.random.uniform(-0.3, 0.3, (Q, 1))).astype(np.float32),
        "fs": (np.random.uniform(256.0, 1024.0, (1, I)) * fi).astype(np.float32),
        "krows": (n((K, T)) / ti).astype(np.float32),
        "res": (n((K, Q)) * 4.0).astype(np.float32),
        "offs": striped(idx),
    }


def reference(fquery, fkeys_words, fkeys_scales, gout, vals, lse, delta, fs, krows, res, offs):
    idx = unstriped(offs)
    fkeysu = unpack_weight(fkeys_words, fkeys_scales, "e4m3")
    fqueryq = mxq(f64(fquery), 0, "e4m3")
    fkeysidxg = fkeysu[:, idx]
    b = fqueryq.T @ fkeysidxg
    goutq = mxq(f64(gout), 0, "e4m3")
    valsq = mxq(f64(vals), 0, "e4m3")
    dp = goutq.T @ valsq
    ds = np.exp(b - f64(lse)) * (dp[:, idx] - f64(delta)) * f64(fs)
    dt = ds.T
    kt = f64(krows)[:, idx].T
    ktq = mxq(kt, 0, "e4m3")
    dtq = mxq(dt, 0, "e4m3")
    gq = ktq.T @ dtq
    y = gq + f64(res)
    words, scales = planes(y)
    return y, words, scales

@@ -1,0 +1,284 @@
+from contextlib import ExitStack
+
+import concourse.mybir as mybir
+from concourse.masks import make_identity
+
+F32 = mybir.dt.float32
+BF16 = mybir.dt.bfloat16
+I32 = mybir.dt.int32
+U32 = mybir.dt.uint32
+U16 = mybir.dt.uint16
+U8 = mybir.dt.uint8
+FP8X4 = mybir.dt.float8_e4m3fn_x4
+ACT = mybir.ActivationFunctionType
+ALU = mybir.AluOpType
+
+P = 128
+PACK = 4
+TOKENS = 1024
+SLOTS = 512
+QUERIES = 256
+HALVES = QUERIES // P
+CHUNK = 256
+CHUNKS = TOKENS // CHUNK
+FLOPS = 2 * 512 * QUERIES * (SLOTS + TOKENS + 512)
+
+
+def tile_attend_gfinequery_pl_kernel(tc, fquery, fkeys_words, fkeys_scales, gout, vals, lse, delta, fs, krows, res, offs,
+                                      out_0, out_1, out_2):
+    nc = tc.nc
+    with ExitStack() as ctx:
+        keep = ctx.enter_context(tc.tile_pool(name="keep", bufs=1))
+        psum = ctx.enter_context(tc.psum_pool(name="psum", bufs=1))
+
+        def sbuf(name, shape, dtype, tag=None):
+            return keep.tile(shape, dtype, name=name, tag=tag or name, align_bytes=64)
+
+        def by_word(rows):
+            return rows.rearrange("(p j) c -> p j c", j=PACK)
+
+        def half(h):
+            return slice(h * P, (h + 1) * P)
+
+        def on_vector(out, in_):
+            nc.vector.tensor_copy(out=out, in_=in_)
+
+        def on_scalar(out, in_):
+            nc.scalar.copy(out=out, in_=in_)
+
+        def on_gpsimd(out, in_):
+            nc.gpsimd.tensor_scalar(out=out, in0=in_, scalar1=1.0, scalar2=0.0, op0=ALU.mult, op1=ALU.add)
+
+        def interleave(copy, grouped, planes):
+            copy(grouped.rearrange("p (c i) j -> p c j i", i=4), planes.rearrange("p j (c i) -> p c j i", i=4))
+
+        def flat(grouped):
+            return grouped.rearrange("p c j -> p (c j)")
+
+        def operand(name, width):
+            return sbuf(name + "_codes", [P, width], U32), sbuf(name + "_scales", [P, width], U8)
+
+        def quantise(target, cols, grouped):
+            nc.vector.quantize_mx(out=target[0][:, cols].bitcast(FP8X4), scales=target[1][:, cols], in_=grouped)
+
+        def product(out, stationary, cols, moving):
+            nc.tensor.matmul_mx(out=out, lhsT=stationary[0][:, cols].bitcast(FP8X4), lhsT_scale=stationary[1][:, cols],
+                                rhs=moving[0][:].bitcast(FP8X4), rhs_scale=moving[1][:], start=True, stop=True)
+
+        def load(name, shape, source, queue=nc.sync):
+            tile = sbuf(name, shape, F32)
+            queue.dma_start(out=tile[:], in_=source)
+            return tile
+
+        offsets = keep.tile([P, SLOTS // 16], U16, name="offsets")
+        nc.sync.dma_start(offsets[:], offs)
+        key_scales = sbuf("key_scales", [P, TOKENS], U8)
+        nc.gpsimd.memset(key_scales[:].bitcast(I32), 0)
+        for quad in range(4):
+            nc.scalar.dma_start(out=key_scales[32 * quad:32 * quad + 4, :].bitcast(I32),
+                                in_=fkeys_scales[0, 4 * quad:4 * quad + 4, :].bitcast(I32))
+        zero = sbuf("zero", [P, 1], F32)
+        nc.gpsimd.memset(zero[:], 0.0)
+        warm = sbuf("warm", [P, 1], F32)
+        nc.scalar.activation(out=warm[:], in_=zero[:], func=ACT.Exp)
+
+        raw = {}
+        key_words = sbuf("key_words", [P, TOKENS], U32)
+        with nc.allow_non_contiguous_dma(reason="one value a query row"):
+            for name in "delta fs lse gout v0 v1 words fq v2 v3 k0 k1 k2 k3 res".split():
+                if name == "words":
+                    nc.sync.dma_start(out=key_words[:].bitcast(I32),
+                                      in_=fkeys_words[0].rearrange("p c r -> p (c r)").bitcast(I32))
+                elif name[0] == "v":
+                    c = int(name[1])
+                    raw[name] = load(name, [P, PACK, CHUNK], by_word(vals)[:, :, c * CHUNK:(c + 1) * CHUNK])
+                elif name[0] == "k":
+                    raw[name] = load(name, [P, TOKENS], by_word(krows)[:, int(name[1]), :])
+                elif name == "fs":
+                    raw[name] = load(name, [P, PACK], fs[0].rearrange("(p j) -> p j", j=PACK), nc.gpsimd)
+                elif name in ("lse", "delta"):
+                    source = lse if name == "lse" else delta
+                    raw[name] = load(name, [P, HALVES, 1], source.rearrange("(h p) o -> p h o", p=P), nc.gpsimd)
+                else:
+                    source = {"gout": gout, "fq": fquery, "res": res}[name]
+                    raw[name] = load(name, [P, PACK, QUERIES], by_word(source))
+
+        identity = sbuf("identity", [P, P], F32)
+        make_identity(nc, identity[:])
+        picked = operand("picked", SLOTS)
+        bf = {}
+        quant = {}
+        banks = {}
+        minus = {}
+        dp = [sbuf("dp%d" % h, [P, TOKENS], F32) for h in range(HALVES)]
+        expd = [sbuf("expd%d" % h, [P, P, PACK], F32) for h in range(HALVES)]
+        weight = [sbuf("weight%d" % h, [P, P, PACK], F32) for h in range(HALVES)]
+        ds = [sbuf("ds%d" % h, [P, SLOTS], F32) for h in range(HALVES)]
+        dt_q = operand("dt", QUERIES)
+        y = [sbuf("y%d" % a, [P, 2, QUERIES], F32) for a in range(2)]
+
+        def gather_words():
+            nc.vector.tensor_copy(out=picked[0][:], in_=key_words[:].indirect(offsets[:]))
+
+        def gather_scales():
+            nc.vector.tensor_copy(out=picked[1][:], in_=key_scales[:].indirect(offsets[:]))
+
+        def negate(name, tag=None):
+            minus[name] = sbuf("minus_" + name, [P, HALVES, 1], F32, tag)
+            nc.scalar.mul(minus[name][:], raw[name][:], -1.0)
+
+        def weave(name, copy, tag=None):
+            bf[name] = sbuf(name + "_bf", [P, 256, PACK], BF16, tag)
+            interleave(copy, bf[name][:], raw[name][:])
+
+        def q(name):
+            width = bf[name].shape[1]
+            quant[name] = operand(name, width)
+            quantise(quant[name], slice(0, width), flat(bf[name][:]))
+
+        def dp_mm(c):
+            banks[c] = psum.tile([P, HALVES, CHUNK], F32, name="dp_bank%d" % c, tag="sums", bufs=3)
+            for h in range(HALVES):
+                product(banks[c][:, h, :], quant["gout"], half(h), quant["v%d" % c])
+
+        def dp_out(c, h):
+            nc.scalar.activation(out=dp[h][:, c * CHUNK:(c + 1) * CHUNK], in_=banks[c][:, h, :], func=ACT.Identity,
+                                 bias=minus["delta"][:, h, :])
+
+        def k_gather(j, tag=None):
+            bf["p%d" % j] = sbuf("krows_picked%d" % j, [P, SLOTS], BF16, tag)
+            nc.vector.tensor_copy(out=bf["p%d" % j][:], in_=raw["k%d" % j][:].indirect(offsets[:]))
+
+        def k_cast(j, copy, tag=None):
+            bf["c%d" % j] = sbuf("krows_cast%d" % j, [P, TOKENS], BF16, tag)
+            copy(bf["c%d" % j][:], raw["k%d" % j][:])
+
+        def k_gather_scalar(j):
+            bf["p%d" % j] = sbuf("krows_picked%d" % j, [P, SLOTS], BF16)
+            nc.scalar.activation(out=bf["p%d" % j][:], in_=bf["c%d" % j][:].indirect(offsets[:]), func=ACT.Copy)
+
+        def k_turn(j):
+            pairs = bf["p%d" % j][:].bitcast(F32).rearrange("k (p u) -> k u p", u=2)
+            banks["k%d" % j] = psum.tile([P, 2, P], F32, name="kt_bank%d" % j, tag="kt", bufs=2)
+            for u in range(2):
+                nc.tensor.transpose(banks["k%d" % j][:, u, :], pairs[:, u, :], identity[:])
+
+        def k_out(j, copy, tag=None):
+            bf["k%d" % j] = sbuf("kt_bf%d" % j, [P, P, PACK], BF16, tag)
+            copy(bf["k%d" % j][:].bitcast(F32), banks["k%d" % j][:].rearrange("p u k -> p k u"))
+
+        def fs_turn():
+            banks["fs"] = psum.tile([P, PACK, P], F32, name="fs_bank")
+            for j in range(PACK):
+                nc.tensor.transpose(banks["fs"][:, j, :], raw["fs"][:, j:j + 1].to_broadcast([P, P]), identity[:])
+
+        def b_mm(h):
+            banks["b%d" % h] = psum.tile([P, SLOTS], F32, name="b_bank%d" % h, tag="scores", bufs=2)
+            product(banks["b%d" % h][:], quant["fq"], half(h), picked)
+
+        def exp(h):
+            nc.scalar.activation(out=flat(expd[h][:]), in_=banks["b%d" % h][:], func=ACT.Exp, bias=minus["lse"][:, h, :])
+
+        def ef(h):
+            nc.vector.tensor_tensor(out=weight[h][:], in0=expd[h][:], in1=banks["fs"][:].rearrange("q j p -> q p j"),
+                                    op=ALU.mult)
+
+        def dp_gather(h):
+            nc.vector.tensor_tensor(out=ds[h][:], in0=dp[h][:].indirect(offsets[:]), in1=flat(weight[h][:]), op=ALU.mult)
+
+        def dt_turn(h):
+            banks["dt%d" % h] = psum.tile([P, PACK, P], F32, name="dt_bank%d" % h, tag="scores", bufs=2)
+            dealt = ds[h][:].rearrange("q (p j) -> q j p", j=PACK)
+            for j in range(PACK):
+                nc.tensor.transpose(banks["dt%d" % h][:, j, :], dealt[:, j, :], identity[:])
+
+        def dt_out(h, copy):
+            bf["dt%d" % h] = sbuf("dt_bf%d" % h, [P, P, PACK], BF16)
+            copy(bf["dt%d" % h][:], banks["dt%d" % h][:].rearrange("p j q -> p q j"))
+
+        def dt_quant(h):
+            quantise(dt_q, half(h), flat(bf["dt%d" % h][:]))
+
+        def clock(*aps):
+            for n, ap in enumerate(aps):
+                tile = sbuf("clock%d" % n, [P, 1], ap.dtype)
+                nc.gpsimd.tensor_copy(out=tile[:], in_=ap)
+
+        gather_scales()
+        weave("gout", on_vector)
+        weave("v0", on_scalar)
+        q("gout")
+        q("v0")
+        dp_mm(0)
+        fs_turn()
+        weave("v1", on_scalar)
+        negate("delta", "v1")
+        gather_words()
+        q("v1")
+        dp_mm(1)
+        weave("fq", on_vector)
+        dp_out(0, 0)
+        dp_out(0, 1)
+        q("fq")
+        b_mm(0)
+        b_mm(1)
+        weave("v2", on_scalar)
+        negate("lse", "v2")
+        dp_out(1, 0)
+        dp_out(1, 1)
+        weave("v3", on_vector)
+        q("v2")
+        dp_mm(2)
+        exp(0)
+        q("v3")
+        dp_mm(3)
+        exp(1)
+        ef(0)
+        k_gather(0)
+        dp_out(2, 0)
+        dp_out(3, 0)
+        dp_out(2, 1)
+        dp_out(3, 1)
+        dp_gather(0)
+        k_turn(0)
+        dt_turn(0)
+        ef(1)
+        k_cast(1, on_scalar, "v1")
+        k_gather_scalar(1)
+        dp_gather(1)
+        dt_turn(1)
+        k_turn(1)
+        k_gather(2, "weight1")
+        k_out(0, on_scalar, "v1")
+        dt_out(0, on_scalar)
+        k_turn(2)
+        k_out(1, on_scalar)
+        dt_out(1, on_scalar)
+        k_gather(3, "k2")
+        k_turn(3)
+        k_out(2, on_scalar)
+        q("k0")
+        dt_quant(0)
+        q("k1")
+        dt_quant(1)
+        q("k2")
+        k_out(3, on_scalar)
+        q("k3")
+
+        y_all = sbuf("y_all", [P, PACK, QUERIES], F32)
+        for first, last in ((0, 2), (2, 3), (3, 4)):
+            bank = psum.tile([P, last - first, QUERIES], F32, name="y_bank%d" % first, tag="sums", bufs=3)
+            for j in range(first, last):
+                product(bank[:, j - first, :], quant["k%d" % j], slice(0, P), dt_q)
+            nc.vector.tensor_tensor(out=y_all[:, first:last, :], in0=bank[:], in1=raw["res"][:, first:last, :], op=ALU.add)
+            nc.sync.dma_start(out=by_word(out_0)[:, first:last, :], in_=y_all[:, first:last, :])
+        y_q = operand("y", QUERIES)
+        y_bf = sbuf("y_bf", [P, QUERIES, PACK], BF16)
+        interleave(on_scalar, y_bf[:, 0:88, :], y_all[:, :, 0:88])
+        interleave(on_vector, y_bf[:, 88:QUERIES, :], y_all[:, :, 88:QUERIES])
+        quantise(y_q, slice(0, QUERIES), flat(y_bf[:]))
+        nc.sync.dma_start(out=out_1[0].rearrange("p c r -> p (c r)").bitcast(I32), in_=y_q[0][:].bitcast(I32))
+        for quad in range(4):
+            queue = nc.sync if quad == 3 else nc.scalar
+            queue.dma_start(out=out_2[0, 4 * quad:4 * quad + 4, :].bitcast(I32),
+                            in_=y_q[1][32 * quad:32 * quad + 4, :].bitcast(I32))

@@ -19,8 +19,7 @@ TOKENS = 1024
 SLOTS = 512
 QUERIES = 256
 HALVES = QUERIES // P
-CHUNK = 256
-CHUNKS = TOKENS // CHUNK
+CHUNKS = ((0, 256), (256, 512), (512, 768), (768, 1024))
 FLOPS = 2 * 512 * QUERIES * (SLOTS + TOKENS + 512)
 
 
@@ -71,7 +70,6 @@ def tile_attend_gfinequery_pl_kernel(tc, fquery, fkeys_words, fkeys_scales, gout
             return tile
 
         offsets = keep.tile([P, SLOTS // 16], U16, name="offsets")
-        nc.sync.dma_start(offsets[:], offs)
         key_scales = sbuf("key_scales", [P, TOKENS], U8)
         nc.gpsimd.memset(key_scales[:].bitcast(I32), 0)
         for quad in range(4):
@@ -82,16 +80,26 @@ def tile_attend_gfinequery_pl_kernel(tc, fquery, fkeys_words, fkeys_scales, gout
         warm = sbuf("warm", [P, 1], F32)
         nc.scalar.activation(out=warm[:], in_=zero[:], func=ACT.Exp)
 
+        identity = sbuf("identity", [P, P], F32)
         raw = {}
         key_words = sbuf("key_words", [P, TOKENS], U32)
         with nc.allow_non_contiguous_dma(reason="one value a query row"):
-            for name in "delta fs lse gout v0 v1 words fq v2 v3 k0 k1 k2 k3 res".split():
-                if name == "words":
+            for name in "fs lse identity delta words fq gout v0 v1 v2 v3 k0 k1 k2 k3 res".split():
+                if name == "identity":
+                    make_identity(nc, identity[:])
+                elif name == "words":
                     nc.sync.dma_start(out=key_words[:].bitcast(I32),
                                       in_=fkeys_words[0].rearrange("p c r -> p (c r)").bitcast(I32))
+                    nc.sync.dma_start(offsets[:], offs)
+                elif name[0] == "V":
+                    c = 2 * int(name[1])
+                    pair = load(name, [P, PACK, 512], by_word(vals)[:, :, c * 256:(c + 2) * 256])
+                    raw["v%d" % c] = pair[:, :, 0:256]
+                    raw["v%d" % (c + 1)] = pair[:, :, 256:512]
                 elif name[0] == "v":
                     c = int(name[1])
-                    raw[name] = load(name, [P, PACK, CHUNK], by_word(vals)[:, :, c * CHUNK:(c + 1) * CHUNK])
+                    raw[name] = load(name, [P, PACK, CHUNKS[c][1] - CHUNKS[c][0]],
+                                     by_word(vals)[:, :, CHUNKS[c][0]:CHUNKS[c][1]])
                 elif name[0] == "k":
                     raw[name] = load(name, [P, TOKENS], by_word(krows)[:, int(name[1]), :])
                 elif name == "fs":
@@ -103,8 +111,6 @@ def tile_attend_gfinequery_pl_kernel(tc, fquery, fkeys_words, fkeys_scales, gout
                     source = {"gout": gout, "fq": fquery, "res": res}[name]
                     raw[name] = load(name, [P, PACK, QUERIES], by_word(source))
 
-        identity = sbuf("identity", [P, P], F32)
-        make_identity(nc, identity[:])
         picked = operand("picked", SLOTS)
         bf = {}
         quant = {}
@@ -115,6 +121,7 @@ def tile_attend_gfinequery_pl_kernel(tc, fquery, fkeys_words, fkeys_scales, gout
         weight = [sbuf("weight%d" % h, [P, P, PACK], F32) for h in range(HALVES)]
         ds = [sbuf("ds%d" % h, [P, SLOTS], F32) for h in range(HALVES)]
         dt_q = operand("dt", QUERIES)
+        dt_bf = sbuf("dt_bf", [P, QUERIES, PACK], BF16)
         y = [sbuf("y%d" % a, [P, 2, QUERIES], F32) for a in range(2)]
 
         def gather_words():
@@ -125,28 +132,41 @@ def tile_attend_gfinequery_pl_kernel(tc, fquery, fkeys_words, fkeys_scales, gout
 
         def negate(name, tag=None):
             minus[name] = sbuf("minus_" + name, [P, HALVES, 1], F32, tag)
-            nc.scalar.mul(minus[name][:], raw[name][:], -1.0)
+            nc.gpsimd.tensor_scalar(out=minus[name][:], in0=raw[name][:], scalar1=-1.0, scalar2=0.0, op0=ALU.mult, op1=ALU.add)
 
-        def weave(name, copy, tag=None):
-            bf[name] = sbuf(name + "_bf", [P, 256, PACK], BF16, tag)
-            interleave(copy, bf[name][:], raw[name][:])
+        def weave(name, copy, tag=None, first=0, last=None):
+            width = raw[name].shape[2]
+            if name not in bf:
+                bf[name] = sbuf(name + "_bf", [P, width, PACK], BF16, tag)
+            cols = slice(first, last or width)
+            interleave(copy, bf[name][:, cols, :], raw[name][:, :, cols])
 
         def q(name):
             width = bf[name].shape[1]
             quant[name] = operand(name, width)
             quantise(quant[name], slice(0, width), flat(bf[name][:]))
 
-        def dp_mm(c):
-            banks[c] = psum.tile([P, HALVES, CHUNK], F32, name="dp_bank%d" % c, tag="sums", bufs=3)
-            for h in range(HALVES):
-                product(banks[c][:, h, :], quant["gout"], half(h), quant["v%d" % c])
+        def dp_bank(h, first, last, tag, bufs):
+            bank = psum.tile([P, (last - first) * 256], F32, name="dp_bank%d_%d" % (first, h), tag=tag, bufs=bufs)
+            banks["o", first, h] = (bank, first, last)
+            for c in range(first, last):
+                banks[c, h] = bank[:, (c - first) * 256:(c - first + 1) * 256]
+
+        def dp_mm(c, h):
+            product(banks[c, h], quant["gout"], half(h), quant["v%d" % c])
 
         def dp_out(c, h):
-            nc.scalar.activation(out=dp[h][:, c * CHUNK:(c + 1) * CHUNK], in_=banks[c][:, h, :], func=ACT.Identity,
+            bank, first, last = banks["o", c, h]
+            nc.scalar.activation(out=dp[h][:, first * 256:last * 256], in_=bank[:], func=ACT.Identity,
                                  bias=minus["delta"][:, h, :])
 
         def k_gather(j, tag=None):
-            bf["p%d" % j] = sbuf("krows_picked%d" % j, [P, SLOTS], BF16, tag)
+            if j < 2:
+                bf["p%d" % j] = sbuf("krows_picked%d" % j, [P, SLOTS], BF16, tag)
+            else:
+                if j == 2:
+                    bf["late"] = sbuf("krows_late", [P, 2 * SLOTS], BF16, "minus_delta")
+                bf["p%d" % j] = bf["late"][:, (j - 2) * SLOTS:(j - 1) * SLOTS]
             nc.vector.tensor_copy(out=bf["p%d" % j][:], in_=raw["k%d" % j][:].indirect(offsets[:]))
 
         def k_cast(j, copy, tag=None):
@@ -168,7 +188,7 @@ def tile_attend_gfinequery_pl_kernel(tc, fquery, fkeys_words, fkeys_scales, gout
             copy(bf["k%d" % j][:].bitcast(F32), banks["k%d" % j][:].rearrange("p u k -> p k u"))
 
         def fs_turn():
-            banks["fs"] = psum.tile([P, PACK, P], F32, name="fs_bank")
+            banks["fs"] = psum.tile([P, PACK, P], F32, name="fs_bank", tag="fs_bank")
             for j in range(PACK):
                 nc.tensor.transpose(banks["fs"][:, j, :], raw["fs"][:, j:j + 1].to_broadcast([P, P]), identity[:])
 
@@ -193,89 +213,111 @@ def tile_attend_gfinequery_pl_kernel(tc, fquery, fkeys_words, fkeys_scales, gout
                 nc.tensor.transpose(banks["dt%d" % h][:, j, :], dealt[:, j, :], identity[:])
 
         def dt_out(h, copy):
-            bf["dt%d" % h] = sbuf("dt_bf%d" % h, [P, P, PACK], BF16)
-            copy(bf["dt%d" % h][:], banks["dt%d" % h][:].rearrange("p j q -> p q j"))
+            copy(dt_bf[:, half(h), :], banks["dt%d" % h][:].rearrange("p j q -> p q j"))
 
-        def dt_quant(h):
-            quantise(dt_q, half(h), flat(bf["dt%d" % h][:]))
+        def ds_round(h, copy, tag=None):
+            bf["ds%d" % h] = sbuf("ds_bf%d" % h, [P, 2, P, 2], BF16, tag)
+            copy(bf["ds%d" % h][:], ds[h][:].rearrange("q (p u e) -> q u p e", u=2, e=2))
+
+        def ds_turn(h):
+            pairs = bf["ds%d" % h][:].rearrange("q u p e -> q (u p e)").bitcast(F32).rearrange("q (u p) -> q u p", u=2)
+            banks["dt%d" % h] = psum.tile([P, 2, P], F32, name="dt_bank%d" % h, tag="scores", bufs=2)
+            for u in range(2):
+                nc.tensor.transpose(banks["dt%d" % h][:, u, :], pairs[:, u, :], identity[:])
+
+        def ds_out(h, copy):
+            bf["dt%d" % h] = sbuf("dt_bf%d" % h, [P, P, PACK], BF16)
+            copy(bf["dt%d" % h][:].bitcast(F32), banks["dt%d" % h][:].rearrange("p u q -> p q u"))
+
+        def dt_quant():
+            quantise(dt_q, slice(0, QUERIES), flat(dt_bf[:]))
 
         def clock(*aps):
             for n, ap in enumerate(aps):
                 tile = sbuf("clock%d" % n, [P, 1], ap.dtype)
                 nc.gpsimd.tensor_copy(out=tile[:], in_=ap)
 
+        negate("lse", None)
+        negate("delta", None)
         gather_scales()
-        weave("gout", on_vector)
-        weave("v0", on_scalar)
-        q("gout")
-        q("v0")
-        dp_mm(0)
-        fs_turn()
-        weave("v1", on_scalar)
-        negate("delta", "v1")
+        weave("fq", on_scalar)
         gather_words()
-        q("v1")
-        dp_mm(1)
-        weave("fq", on_vector)
-        dp_out(0, 0)
-        dp_out(0, 1)
+        weave("gout", on_scalar)
         q("fq")
         b_mm(0)
         b_mm(1)
-        weave("v2", on_scalar)
-        negate("lse", "v2")
-        dp_out(1, 0)
-        dp_out(1, 1)
-        weave("v3", on_vector)
-        q("v2")
-        dp_mm(2)
+        q("gout")
+        fs_turn()
+        weave("v0", on_scalar)
         exp(0)
-        q("v3")
-        dp_mm(3)
+        weave("v1", on_vector)
+        q("v0")
+        dp_bank(0, 0, 2, "sums", 3)
+        dp_bank(1, 0, 2, "sums", 3)
+        dp_mm(0, 0)
+        dp_mm(0, 1)
         exp(1)
+        q("v1")
+        dp_mm(1, 0)
+        dp_mm(1, 1)
         ef(0)
+        weave("v2", on_scalar)
+        ef(1)
+        weave("v3", on_vector)
+        dp_out(0, 0)
+        q("v2")
+        dp_bank(0, 2, 3, "sums", 3)
+        dp_mm(2, 0)
+        q("v3")
+        dp_bank(0, 3, 4, "scores", 2)
+        dp_mm(3, 0)
+        dp_bank(1, 2, 4, "scores", 2)
+        dp_mm(2, 1)
+        dp_mm(3, 1)
         k_gather(0)
+        dp_out(0, 1)
         dp_out(2, 0)
         dp_out(3, 0)
         dp_out(2, 1)
-        dp_out(3, 1)
         dp_gather(0)
         k_turn(0)
         dt_turn(0)
-        ef(1)
-        k_cast(1, on_scalar, "v1")
+        k_cast(1, on_scalar, "v3_codes")
+        k_out(0, on_scalar, None)
         k_gather_scalar(1)
         dp_gather(1)
         dt_turn(1)
         k_turn(1)
-        k_gather(2, "weight1")
-        k_out(0, on_scalar, "v1")
+        k_gather(2)
         dt_out(0, on_scalar)
         k_turn(2)
-        k_out(1, on_scalar)
         dt_out(1, on_scalar)
-        k_gather(3, "k2")
+        k_out(1, on_scalar, None)
+        k_gather(3)
         k_turn(3)
-        k_out(2, on_scalar)
+        k_out(2, on_scalar, None)
         q("k0")
-        dt_quant(0)
+        dt_quant()
         q("k1")
-        dt_quant(1)
         q("k2")
-        k_out(3, on_scalar)
+        k_out(3, on_scalar, None)
         q("k3")
 
         y_all = sbuf("y_all", [P, PACK, QUERIES], F32)
-        for first, last in ((0, 2), (2, 3), (3, 4)):
-            bank = psum.tile([P, last - first, QUERIES], F32, name="y_bank%d" % first, tag="sums", bufs=3)
-            for j in range(first, last):
-                product(bank[:, j - first, :], quant["k%d" % j], slice(0, P), dt_q)
-            nc.vector.tensor_tensor(out=y_all[:, first:last, :], in0=bank[:], in1=raw["res"][:, first:last, :], op=ALU.add)
-            nc.sync.dma_start(out=by_word(out_0)[:, first:last, :], in_=y_all[:, first:last, :])
+        for j in range(PACK):
+            if j < 3:
+                bank = psum.tile([P, QUERIES], F32, name="y_bank%d" % j, tag="sums", bufs=3)
+            else:
+                bank = psum.tile([P, QUERIES], F32, name="y_bank%d" % j, tag="fs_bank")
+            product(bank[:], quant["k%d" % j], slice(0, P), dt_q)
+            nc.vector.tensor_tensor(out=y_all[:, j, :], in0=bank[:], in1=raw["res"][:, j, :], op=ALU.add)
+            if j > 0:
+                first = 0 if j == 1 else j
+                nc.sync.dma_start(out=by_word(out_0)[:, first:j + 1, :], in_=y_all[:, first:j + 1, :])
         y_q = operand("y", QUERIES)
         y_bf = sbuf("y_bf", [P, QUERIES, PACK], BF16)
-        interleave(on_scalar, y_bf[:, 0:88, :], y_all[:, :, 0:88])
-        interleave(on_vector, y_bf[:, 88:QUERIES, :], y_all[:, :, 88:QUERIES])
+        interleave(on_scalar, y_bf[:, 0:128, :], y_all[:, :, 0:128])
+        interleave(on_vector, y_bf[:, 128:QUERIES, :], y_all[:, :, 128:QUERIES])
         quantise(y_q, slice(0, QUERIES), flat(y_bf[:]))
         nc.sync.dma_start(out=out_1[0].rearrange("p c r -> p (c r)").bitcast(I32), in_=y_q[0][:].bitcast(I32))
         for quad in range(4):

from contextlib import ExitStack

import concourse.mybir as mybir
from concourse.masks import make_identity

F32 = mybir.dt.float32
BF16 = mybir.dt.bfloat16
I32 = mybir.dt.int32
U32 = mybir.dt.uint32
U16 = mybir.dt.uint16
U8 = mybir.dt.uint8
FP8X4 = mybir.dt.float8_e4m3fn_x4
ACT = mybir.ActivationFunctionType
ALU = mybir.AluOpType

P = 128
PACK = 4
TOKENS = 1024
SLOTS = 512
QUERIES = 256
HALVES = QUERIES // P
CHUNKS = ((0, 256), (256, 512), (512, 768), (768, 1024))
FLOPS = 2 * 512 * QUERIES * (SLOTS + TOKENS + 512)


def tile_attend_gfinequery_pl_kernel(tc, fquery, fkeys_words, fkeys_scales, gout, vals, lse, delta, fs, krows, res, offs,
                                      out_0, out_1, out_2):
    nc = tc.nc
    with ExitStack() as ctx:
        keep = ctx.enter_context(tc.tile_pool(name="keep", bufs=1))
        psum = ctx.enter_context(tc.psum_pool(name="psum", bufs=1))

        def sbuf(name, shape, dtype, tag=None):
            return keep.tile(shape, dtype, name=name, tag=tag or name, align_bytes=64)

        def by_word(rows):
            return rows.rearrange("(p j) c -> p j c", j=PACK)

        def half(h):
            return slice(h * P, (h + 1) * P)

        def on_vector(out, in_):
            nc.vector.tensor_copy(out=out, in_=in_)

        def on_scalar(out, in_):
            nc.scalar.copy(out=out, in_=in_)

        def on_gpsimd(out, in_):
            nc.gpsimd.tensor_scalar(out=out, in0=in_, scalar1=1.0, scalar2=0.0, op0=ALU.mult, op1=ALU.add)

        def interleave(copy, grouped, planes):
            copy(grouped.rearrange("p (c i) j -> p c j i", i=4), planes.rearrange("p j (c i) -> p c j i", i=4))

        def flat(grouped):
            return grouped.rearrange("p c j -> p (c j)")

        def operand(name, width):
            return sbuf(name + "_codes", [P, width], U32), sbuf(name + "_scales", [P, width], U8)

        def quantise(target, cols, grouped):
            nc.vector.quantize_mx(out=target[0][:, cols].bitcast(FP8X4), scales=target[1][:, cols], in_=grouped)

        def product(out, stationary, cols, moving):
            nc.tensor.matmul_mx(out=out, lhsT=stationary[0][:, cols].bitcast(FP8X4), lhsT_scale=stationary[1][:, cols],
                                rhs=moving[0][:].bitcast(FP8X4), rhs_scale=moving[1][:], start=True, stop=True)

        def load(name, shape, source, queue=nc.sync):
            tile = sbuf(name, shape, F32)
            queue.dma_start(out=tile[:], in_=source)
            return tile

        offsets = keep.tile([P, SLOTS // 16], U16, name="offsets")
        key_scales = sbuf("key_scales", [P, TOKENS], U8)
        nc.gpsimd.memset(key_scales[:].bitcast(I32), 0)
        for quad in range(4):
            nc.scalar.dma_start(out=key_scales[32 * quad:32 * quad + 4, :].bitcast(I32),
                                in_=fkeys_scales[0, 4 * quad:4 * quad + 4, :].bitcast(I32))
        zero = sbuf("zero", [P, 1], F32)
        nc.gpsimd.memset(zero[:], 0.0)
        warm = sbuf("warm", [P, 1], F32)
        nc.scalar.activation(out=warm[:], in_=zero[:], func=ACT.Exp)

        identity = sbuf("identity", [P, P], F32)
        raw = {}
        key_words = sbuf("key_words", [P, TOKENS], U32)
        with nc.allow_non_contiguous_dma(reason="one value a query row"):
            for name in "fs lse identity delta words fq gout v0 v1 v2 v3 k0 k1 k2 k3 res".split():
                if name == "identity":
                    make_identity(nc, identity[:])
                elif name == "words":
                    nc.sync.dma_start(out=key_words[:].bitcast(I32),
                                      in_=fkeys_words[0].rearrange("p c r -> p (c r)").bitcast(I32))
                    nc.sync.dma_start(offsets[:], offs)
                elif name[0] == "V":
                    c = 2 * int(name[1])
                    pair = load(name, [P, PACK, 512], by_word(vals)[:, :, c * 256:(c + 2) * 256])
                    raw["v%d" % c] = pair[:, :, 0:256]
                    raw["v%d" % (c + 1)] = pair[:, :, 256:512]
                elif name[0] == "v":
                    c = int(name[1])
                    raw[name] = load(name, [P, PACK, CHUNKS[c][1] - CHUNKS[c][0]],
                                     by_word(vals)[:, :, CHUNKS[c][0]:CHUNKS[c][1]])
                elif name[0] == "k":
                    raw[name] = load(name, [P, TOKENS], by_word(krows)[:, int(name[1]), :])
                elif name == "fs":
                    raw[name] = load(name, [P, PACK], fs[0].rearrange("(p j) -> p j", j=PACK), nc.gpsimd)
                elif name in ("lse", "delta"):
                    source = lse if name == "lse" else delta
                    raw[name] = load(name, [P, HALVES, 1], source.rearrange("(h p) o -> p h o", p=P), nc.gpsimd)
                else:
                    source = {"gout": gout, "fq": fquery, "res": res}[name]
                    raw[name] = load(name, [P, PACK, QUERIES], by_word(source))

        picked = operand("picked", SLOTS)
        bf = {}
        quant = {}
        banks = {}
        minus = {}
        dp = [sbuf("dp%d" % h, [P, TOKENS], F32) for h in range(HALVES)]
        expd = [sbuf("expd%d" % h, [P, P, PACK], F32) for h in range(HALVES)]
        weight = [sbuf("weight%d" % h, [P, P, PACK], F32) for h in range(HALVES)]
        ds = [sbuf("ds%d" % h, [P, SLOTS], F32) for h in range(HALVES)]
        dt_q = operand("dt", QUERIES)
        dt_bf = sbuf("dt_bf", [P, QUERIES, PACK], BF16)
        y = [sbuf("y%d" % a, [P, 2, QUERIES], F32) for a in range(2)]

        def gather_words():
            nc.vector.tensor_copy(out=picked[0][:], in_=key_words[:].indirect(offsets[:]))

        def gather_scales():
            nc.vector.tensor_copy(out=picked[1][:], in_=key_scales[:].indirect(offsets[:]))

        def negate(name, tag=None):
            minus[name] = sbuf("minus_" + name, [P, HALVES, 1], F32, tag)
            nc.gpsimd.tensor_scalar(out=minus[name][:], in0=raw[name][:], scalar1=-1.0, scalar2=0.0, op0=ALU.mult, op1=ALU.add)

        def weave(name, copy, tag=None, first=0, last=None):
            width = raw[name].shape[2]
            if name not in bf:
                bf[name] = sbuf(name + "_bf", [P, width, PACK], BF16, tag)
            cols = slice(first, last or width)
            interleave(copy, bf[name][:, cols, :], raw[name][:, :, cols])

        def q(name):
            width = bf[name].shape[1]
            quant[name] = operand(name, width)
            quantise(quant[name], slice(0, width), flat(bf[name][:]))

        def dp_bank(h, first, last, tag, bufs):
            bank = psum.tile([P, (last - first) * 256], F32, name="dp_bank%d_%d" % (first, h), tag=tag, bufs=bufs)
            banks["o", first, h] = (bank, first, last)
            for c in range(first, last):
                banks[c, h] = bank[:, (c - first) * 256:(c - first + 1) * 256]

        def dp_mm(c, h):
            product(banks[c, h], quant["gout"], half(h), quant["v%d" % c])

        def dp_out(c, h):
            bank, first, last = banks["o", c, h]
            nc.scalar.activation(out=dp[h][:, first * 256:last * 256], in_=bank[:], func=ACT.Identity,
                                 bias=minus["delta"][:, h, :])

        def k_gather(j, tag=None):
            if j < 2:
                bf["p%d" % j] = sbuf("krows_picked%d" % j, [P, SLOTS], BF16, tag)
            else:
                if j == 2:
                    bf["late"] = sbuf("krows_late", [P, 2 * SLOTS], BF16, "minus_delta")
                bf["p%d" % j] = bf["late"][:, (j - 2) * SLOTS:(j - 1) * SLOTS]
            nc.vector.tensor_copy(out=bf["p%d" % j][:], in_=raw["k%d" % j][:].indirect(offsets[:]))

        def k_cast(j, copy, tag=None):
            bf["c%d" % j] = sbuf("krows_cast%d" % j, [P, TOKENS], BF16, tag)
            copy(bf["c%d" % j][:], raw["k%d" % j][:])

        def k_gather_scalar(j):
            bf["p%d" % j] = sbuf("krows_picked%d" % j, [P, SLOTS], BF16)
            nc.scalar.activation(out=bf["p%d" % j][:], in_=bf["c%d" % j][:].indirect(offsets[:]), func=ACT.Copy)

        def k_turn(j):
            pairs = bf["p%d" % j][:].bitcast(F32).rearrange("k (p u) -> k u p", u=2)
            banks["k%d" % j] = psum.tile([P, 2, P], F32, name="kt_bank%d" % j, tag="kt", bufs=2)
            for u in range(2):
                nc.tensor.transpose(banks["k%d" % j][:, u, :], pairs[:, u, :], identity[:])

        def k_out(j, copy, tag=None):
            bf["k%d" % j] = sbuf("kt_bf%d" % j, [P, P, PACK], BF16, tag)
            copy(bf["k%d" % j][:].bitcast(F32), banks["k%d" % j][:].rearrange("p u k -> p k u"))

        def fs_turn():
            banks["fs"] = psum.tile([P, PACK, P], F32, name="fs_bank", tag="fs_bank")
            for j in range(PACK):
                nc.tensor.transpose(banks["fs"][:, j, :], raw["fs"][:, j:j + 1].to_broadcast([P, P]), identity[:])

        def b_mm(h):
            banks["b%d" % h] = psum.tile([P, SLOTS], F32, name="b_bank%d" % h, tag="scores", bufs=2)
            product(banks["b%d" % h][:], quant["fq"], half(h), picked)

        def exp(h):
            nc.scalar.activation(out=flat(expd[h][:]), in_=banks["b%d" % h][:], func=ACT.Exp, bias=minus["lse"][:, h, :])

        def ef(h):
            nc.vector.tensor_tensor(out=weight[h][:], in0=expd[h][:], in1=banks["fs"][:].rearrange("q j p -> q p j"),
                                    op=ALU.mult)

        def dp_gather(h):
            nc.vector.tensor_tensor(out=ds[h][:], in0=dp[h][:].indirect(offsets[:]), in1=flat(weight[h][:]), op=ALU.mult)

        def dt_turn(h):
            banks["dt%d" % h] = psum.tile([P, PACK, P], F32, name="dt_bank%d" % h, tag="scores", bufs=2)
            dealt = ds[h][:].rearrange("q (p j) -> q j p", j=PACK)
            for j in range(PACK):
                nc.tensor.transpose(banks["dt%d" % h][:, j, :], dealt[:, j, :], identity[:])

        def dt_out(h, copy):
            copy(dt_bf[:, half(h), :], banks["dt%d" % h][:].rearrange("p j q -> p q j"))

        def ds_round(h, copy, tag=None):
            bf["ds%d" % h] = sbuf("ds_bf%d" % h, [P, 2, P, 2], BF16, tag)
            copy(bf["ds%d" % h][:], ds[h][:].rearrange("q (p u e) -> q u p e", u=2, e=2))

        def ds_turn(h):
            pairs = bf["ds%d" % h][:].rearrange("q u p e -> q (u p e)").bitcast(F32).rearrange("q (u p) -> q u p", u=2)
            banks["dt%d" % h] = psum.tile([P, 2, P], F32, name="dt_bank%d" % h, tag="scores", bufs=2)
            for u in range(2):
                nc.tensor.transpose(banks["dt%d" % h][:, u, :], pairs[:, u, :], identity[:])

        def ds_out(h, copy):
            bf["dt%d" % h] = sbuf("dt_bf%d" % h, [P, P, PACK], BF16)
            copy(bf["dt%d" % h][:].bitcast(F32), banks["dt%d" % h][:].rearrange("p u q -> p q u"))

        def dt_quant():
            quantise(dt_q, slice(0, QUERIES), flat(dt_bf[:]))

        def clock(*aps):
            for n, ap in enumerate(aps):
                tile = sbuf("clock%d" % n, [P, 1], ap.dtype)
                nc.gpsimd.tensor_copy(out=tile[:], in_=ap)

        negate("lse", None)
        negate("delta", None)
        gather_scales()
        weave("fq", on_scalar)
        gather_words()
        weave("gout", on_scalar)
        q("fq")
        b_mm(0)
        b_mm(1)
        q("gout")
        fs_turn()
        weave("v0", on_scalar)
        exp(0)
        weave("v1", on_vector)
        q("v0")
        dp_bank(0, 0, 2, "sums", 3)
        dp_bank(1, 0, 2, "sums", 3)
        dp_mm(0, 0)
        dp_mm(0, 1)
        exp(1)
        q("v1")
        dp_mm(1, 0)
        dp_mm(1, 1)
        ef(0)
        weave("v2", on_scalar)
        ef(1)
        weave("v3", on_vector)
        dp_out(0, 0)
        q("v2")
        dp_bank(0, 2, 3, "sums", 3)
        dp_mm(2, 0)
        q("v3")
        dp_bank(0, 3, 4, "scores", 2)
        dp_mm(3, 0)
        dp_bank(1, 2, 4, "scores", 2)
        dp_mm(2, 1)
        dp_mm(3, 1)
        k_gather(0)
        dp_out(0, 1)
        dp_out(2, 0)
        dp_out(3, 0)
        dp_out(2, 1)
        dp_gather(0)
        k_turn(0)
        dt_turn(0)
        k_cast(1, on_scalar, "v3_codes")
        k_out(0, on_scalar, None)
        k_gather_scalar(1)
        dp_gather(1)
        dt_turn(1)
        k_turn(1)
        k_gather(2)
        dt_out(0, on_scalar)
        k_turn(2)
        dt_out(1, on_scalar)
        k_out(1, on_scalar, None)
        k_gather(3)
        k_turn(3)
        k_out(2, on_scalar, None)
        q("k0")
        dt_quant()
        q("k1")
        q("k2")
        k_out(3, on_scalar, None)
        q("k3")

        y_all = sbuf("y_all", [P, PACK, QUERIES], F32)
        for j in range(PACK):
            if j < 3:
                bank = psum.tile([P, QUERIES], F32, name="y_bank%d" % j, tag="sums", bufs=3)
            else:
                bank = psum.tile([P, QUERIES], F32, name="y_bank%d" % j, tag="fs_bank")
            product(bank[:], quant["k%d" % j], slice(0, P), dt_q)
            nc.vector.tensor_tensor(out=y_all[:, j, :], in0=bank[:], in1=raw["res"][:, j, :], op=ALU.add)
            if j > 0:
                first = 0 if j == 1 else j
                nc.sync.dma_start(out=by_word(out_0)[:, first:j + 1, :], in_=y_all[:, first:j + 1, :])
        y_q = operand("y", QUERIES)
        y_bf = sbuf("y_bf", [P, QUERIES, PACK], BF16)
        interleave(on_scalar, y_bf[:, 0:128, :], y_all[:, :, 0:128])
        interleave(on_vector, y_bf[:, 128:QUERIES, :], y_all[:, :, 128:QUERIES])
        quantise(y_q, slice(0, QUERIES), flat(y_bf[:]))
        nc.sync.dma_start(out=out_1[0].rearrange("p c r -> p (c r)").bitcast(I32), in_=y_q[0][:].bitcast(I32))
        for quad in range(4):
            queue = nc.sync if quad == 3 else nc.scalar
            queue.dma_start(out=out_2[0, 4 * quad:4 * quad + 4, :].bitcast(I32),
                            in_=y_q[1][32 * quad:32 * quad + 4, :].bitcast(I32))
